import numpy as np
import ml_dtypes


def mxq(x, axis, fmt="e4m3"):
    dtype, down = {"e4m3": (ml_dtypes.float8_e4m3fn, 7), "e5m2": (ml_dtypes.float8_e5m2, 14)}[fmt]
    v = np.moveaxis(np.asarray(x, np.float32).astype(ml_dtypes.bfloat16).astype(np.float64), axis, -1)
    blocks = v.reshape(v.shape[:-1] + (-1, 32))
    amax = np.abs(blocks).max(-1, keepdims=True)
    byte = np.maximum(np.where(amax > 0, np.frexp(amax)[1] - 1 + 127, 0) - down, 1)
    scale = np.exp2(byte - 127.0)
    codes = (blocks / scale).astype(np.float32).astype(dtype).astype(np.float64)
    return np.moveaxis((codes * scale).reshape(v.shape), -1, axis)


WIDE = False


def mx_kscale(k):
    if not WIDE:
        return np.ones(k)
    levels = np.array([10, -10, 5, -5, 0])
    if k % 512:
        return np.exp2(np.random.permutation(np.resize(levels, k // 32))).repeat(32)
    a = np.empty((k // 512, 16))
    for p in range(k // 512):
        a[p, :8] = np.random.permutation(np.resize(levels, 8))
        for g in range(8):
            far = levels[np.abs(levels - a[p, g]) >= 10]
            a[p, g + 8] = far[np.random.randint(len(far))]
    return np.exp2(a.ravel()).repeat(32)


def f64(x):
    return np.asarray(x).astype(np.float64)


def striped(idx):
    return np.tile(idx.reshape(-1, 16).T, (8, 1)).astype(np.uint16)


def unstriped(offs):
    return offs[:16].T.reshape(-1).astype(np.int64)


def striped8(idx):
    return np.concatenate([x.reshape(-1, 16).T for x in idx]).astype(np.uint16)


def runs(offs, k):
    lists = np.stack([offs[16 * r : 16 * r + 16].T.reshape(-1) for r in range(8)]).astype(np.int64)
    return lists[np.arange(k) % 512 // 64]


def pack_weight(w):
    k, n = w.shape
    w = f64(np.asarray(w, np.float32).astype(ml_dtypes.bfloat16)).reshape(k // 32, 32, n)
    amax = np.abs(w).max(1)
    byte = np.clip(np.where(amax > 0, np.frexp(amax)[1] - 1 + 127 - 7, 1), 1, 254)
    scaled = (w * np.exp2(127.0 - byte)[:, None, :]).reshape(k, n).astype(np.float32)
    words = np.ascontiguousarray(scaled.reshape(k // 512, 128, 4, n).transpose(0, 1, 3, 2)).astype(ml_dtypes.float8_e4m3fn).view(np.uint8)
    return words, np.ascontiguousarray(byte.astype(np.uint8).reshape(k // 512, 16, n))


def unpack_weight(words, scales):
    g, p, n, _ = words.shape
    vals = np.ascontiguousarray(words).view(ml_dtypes.float8_e4m3fn).astype(np.float64) * np.repeat(np.exp2(scales.astype(np.float64) - 127.0), 8, axis=1)[..., None]
    return vals.transpose(0, 1, 3, 2).reshape(g * 512, n)


def sigmoid(v):
    return 1.0 / (1.0 + np.exp(-np.maximum(v, -700.0)))


K, T, S, G, H, U = 512, 1024, 256, 2048, 512, 512


def setup_inputs():
    n = np.random.standard_normal
    s = mx_kscale(K)[:, None]
    packed_xT = pack_weight(n((K, T)) * s)
    packed_dT = pack_weight(n((K, G)) / s)
    perm = np.random.permutation(U)
    return {
        "x_words": packed_xT[0],
        "x_scales": packed_xT[1],
        "d_words": packed_dT[0],
        "d_scales": packed_dT[1],
        "gs": (np.random.uniform(0.5, 1.5, (K, 1)) * s).astype(np.float32),
        "offs": striped8(np.random.randint(0, T, (8, S))),
        "ci": striped(np.random.permutation(G)[:H]),
        "n1": striped8(np.stack([np.random.permutation(S) for _ in range(8)])),
        "n2": striped8(np.stack([np.random.permutation(S) for _ in range(8)])),
        "k1": striped8(np.random.randint(0, G, (8, H))),
        "n3": striped(perm[:S]),
        "n4": striped(perm[S:]),
        "n5": striped(np.random.permutation(S)),
    }


def reference(x_words, x_scales, d_words, d_scales, gs, offs, ci, n1, n2, k1, n3, n4, n5):
    d_k1 = unpack_weight(d_words, d_scales)[np.arange(K)[:, None], runs(k1, K)]
    d_ci = unpack_weight(d_words, d_scales)[:, unstriped(ci)]
    xq = unpack_weight(x_words, x_scales)[np.arange(K)[:, None], runs(offs, K)]
    s = 0.0625 * (d_ci.T @ xq)
    st = s[np.arange(H)[:, None], runs(n1, H)] - s
    z = f64(gs) * (s * (sigmoid(st[np.arange(H)[:, None], runs(n2, H)])))
    h = 0.0625 * ((d_k1.T @ mxq(z, 0, "e4m3")))
    nw = h - h[:, unstriped(n5)]
    ph = np.zeros((H, U))
    ph[:, unstriped(n3)] = h
    out = ph.copy()
    out[:, unstriped(n4)] = nw
    return out

@@ -1,0 +1,226 @@
+from contextlib import ExitStack
+
+import concourse.mybir as mybir
+
+F32 = mybir.dt.float32
+BF16 = mybir.dt.bfloat16
+I32 = mybir.dt.int32
+U32 = mybir.dt.uint32
+U16 = mybir.dt.uint16
+U8 = mybir.dt.uint8
+FP8X4 = mybir.dt.float8_e4m3fn_x4
+ALU = mybir.AluOpType
+ACT = mybir.ActivationFunctionType
+
+P = 128
+PACK = 4
+T, S, G, H, U = 1024, 256, 2048, 512, 512
+HALF = S // 2
+PER_COL = 16
+WIDE = 2 * S
+H_WIDE = S + 16
+SIXTEENTH = 0.0625
+MX = 64
+
+FLOPS = 2 * 2 * 512 * H * S
+
+
+def entries(lst, start, stop):
+    return lst[:, start // PER_COL : stop // PER_COL]
+
+
+def place_scale_rows(queue, placed, picked):
+    for r in range(4):
+        queue.dma_start(out=placed[:].bitcast(I32)[r:P:32, :], in_=picked[:].bitcast(I32)[8 * r : P : 32, :])
+
+
+def product(nc, acc, words, scales, moving, moving_scales):
+    nc.tensor.matmul_mx(
+        out=acc,
+        lhsT=words.bitcast(FP8X4),
+        lhsT_scale=scales,
+        rhs=moving.bitcast(FP8X4),
+        rhs_scale=moving_scales,
+        start=True,
+        stop=True,
+    )
+
+
+def tile_picked_hwqhopdpagq_none_p_kernel(
+    tc, x_words, x_scales, d_words, d_scales, gs, offs, ci, n1, n2, k1, n3, n4, n5, out
+):
+    nc = tc.nc
+    with ExitStack() as ctx:
+        lists = ctx.enter_context(tc.tile_pool(name="lists", bufs=1))
+        sb = ctx.enter_context(tc.tile_pool(name="sb", bufs=1))
+        psum = ctx.enter_context(tc.psum_pool(name="psum", bufs=8))
+
+        def load_list(src, name):
+            lst = lists.tile(list(src.shape), U16, name=name)
+            nc.sync.dma_start(lst[:], src)
+            return lst
+
+        x_rows = sb.tile([P, T], U8)
+        d_rows_ci = sb.tile([P, G], U8)
+        d_rows_k1 = sb.tile([P, G], U8)
+        x_placed = sb.tile([P, S], U8, align_bytes=MX)
+        k_placed = [sb.tile([P, S], U8, name=f"k_placed{u}", align_bytes=MX) for u in range(2)]
+        for zeroed in [x_rows, d_rows_ci, d_rows_k1, x_placed] + k_placed:
+            nc.vector.memset(zeroed[:].bitcast(I32), 0)
+
+        s_win = [sb.tile([P, WIDE], F32, name=f"s_win{t}") for t in range(PACK)]
+        st_win = [sb.tile([P, WIDE], F32, name=f"st_win{t}") for t in range(PACK)]
+        h_win = [sb.tile([P, H_WIDE], F32, name=f"h_win{b}") for b in range(PACK)]
+        for win in s_win + st_win + h_win:
+            nc.vector.memset(win[:, S:], 0.0)
+
+        offs_l = load_list(offs, "offs_l")
+        ci_l = load_list(ci, "ci_l")
+        nc.scalar.dma_start(out=x_rows[:].bitcast(I32)[0:P:8, :], in_=x_scales[0].bitcast(I32))
+        for q in range(4):
+            nc.scalar.dma_start(
+                out=d_rows_ci[:].bitcast(I32)[32 * q : 32 * q + 4, :],
+                in_=d_scales[0].bitcast(I32)[4 * q : 4 * q + 4, :],
+            )
+        d_tab = sb.tile([P, G], U32)
+        nc.sync.dma_start(out=d_tab[:].bitcast(I32), in_=d_words[0].rearrange("p n t -> p (n t)").bitcast(I32))
+        x_tab = sb.tile([P, T], U32)
+        nc.sync.dma_start(out=x_tab[:].bitcast(I32), in_=x_words[0].rearrange("p n t -> p (n t)").bitcast(I32))
+        n1_l = load_list(n1, "n1_l")
+        k1_l = load_list(k1, "k1_l")
+        nc.sync.dma_start(out=d_rows_k1[:].bitcast(I32)[0:P:8, :], in_=d_scales[0].bitcast(I32))
+        n2_l = load_list(n2, "n2_l")
+        gs_t = sb.tile([P, PACK], F32)
+        nc.sync.dma_start(out=gs_t[:], in_=gs.rearrange("(p t) o -> p (t o)", t=PACK))
+        n5_l = load_list(n5, "n5_l")
+        n3_l = load_list(n3, "n3_l")
+        n4_l = load_list(n4, "n4_l")
+
+        x_picked = sb.tile([P, S], U8)
+        nc.vector.tensor_copy(x_picked[:], x_rows[:].indirect(offs_l[:]))
+        place_scale_rows(nc.scalar, x_placed, x_picked)
+
+        c_bytes = sb.tile([P, H], U8)
+        nc.vector.tensor_copy(c_bytes[:], d_rows_ci[:].indirect(ci_l[:]))
+        c_bytes_dealt = sb.tile([P, H], U8, align_bytes=MX)
+        nc.vector.tensor_copy(
+            c_bytes_dealt[:].rearrange("p (t c i) -> p c t i", t=PACK, i=16),
+            c_bytes[:].rearrange("p (c i t) -> p c t i", t=PACK, i=16),
+        )
+        c_words = sb.tile([P, H], U32)
+        nc.vector.tensor_copy(c_words[:], d_tab[:].indirect(ci_l[:]))
+        c_words_dealt = sb.tile([P, H], U32, align_bytes=MX)
+        nc.vector.tensor_copy(
+            c_words_dealt[:].rearrange("p (t c i) -> p c t i", t=PACK, i=4),
+            c_words[:].rearrange("p (c i t) -> p c t i", t=PACK, i=4),
+        )
+        xq_words = sb.tile([P, S], U32, align_bytes=MX)
+        nc.vector.tensor_copy(xq_words[:], x_tab[:].indirect(offs_l[:]))
+
+        s_at_n1 = sb.tile([P, PACK, S], F32, tag="looked_up")
+        for t in range(PACK):
+            cols = slice(P * t, P * (t + 1))
+            acc = psum.tile([P, S], F32, name="acc")
+            product(nc, acc[:], c_words_dealt[:, cols], c_bytes_dealt[:, cols], xq_words[:], x_placed[:])
+            nc.vector.tensor_scalar(s_win[t][:, :S], acc[:], SIXTEENTH, None, ALU.mult)
+            nc.scalar.activation(s_at_n1[:, t, :], s_win[t][:].indirect(n1_l[:]), ACT.Copy)
+
+        def pick_k1_bytes(u, tag):
+            picked = sb.tile([P, S], U8, name=f"k_picked{u}", tag=tag, align_bytes=MX)
+            nc.vector.tensor_copy(picked[:], d_rows_k1[:].indirect(entries(k1_l, S * u, S * (u + 1))))
+            place_scale_rows(nc.sync, k_placed[u], picked)
+
+        def pick_k1_words(u, tag):
+            picked = sb.tile([P, S], U32, name=f"k_words{u}", tag=tag, align_bytes=MX)
+            nc.vector.tensor_copy(picked[:], d_tab[:].indirect(entries(k1_l, S * u, S * (u + 1))))
+            return picked
+
+        def subtract_s(t):
+            nc.vector.tensor_tensor(st_win[t][:, :S], s_at_n1[:, t, :], s_win[t][:, :S], ALU.subtract)
+
+        pick_k1_bytes(0, "k_picked0")
+        subtract_s(0)
+        subtract_s(1)
+        k_words = [pick_k1_words(0, "k_words0")]
+        subtract_s(2)
+        subtract_s(3)
+
+        gates = []
+        for u, tag in enumerate(["gate0", "looked_up"]):
+            gate = sb.tile([P, PACK, HALF], F32, name=f"gate{u}", tag=tag)
+            for t in range(PACK):
+                nc.scalar.activation(
+                    gate[:, t, :], st_win[t][:].indirect(entries(n2_l, HALF * u, HALF * (u + 1))), ACT.Sigmoid
+                )
+            gates.append(gate)
+
+        z_words = sb.tile([P, S], U32, align_bytes=MX)
+        z_scales = sb.tile([P, S], U8, align_bytes=MX)
+        page = [sb.tile([P, U], F32, name=f"page{b}") for b in range(PACK)]
+
+        def make_h(b, start, stop):
+            cols = slice(P * (b % 2), P * (b % 2 + 1))
+            acc = psum.tile([P, S], F32, name="acc")
+            product(
+                nc,
+                acc[:, : stop - start],
+                k_words[b // 2][:, cols],
+                k_placed[b // 2][:, cols],
+                z_words[:, start:stop],
+                z_scales[:, start:stop],
+            )
+            nc.vector.tensor_scalar(h_win[b][:, start:stop], acc[:, : stop - start], SIXTEENTH, None, ALU.mult)
+
+        def put_h(b, start, stop):
+            nc.scalar.activation(page[b][:].indirect(entries(n3_l, start, stop)), h_win[b][:, start:stop], ACT.Copy)
+
+        def make_nw(b):
+            h_at_n5 = sb.tile([P, S], F32, name=f"h_at_n5_{b}", tag=f"h_at_n5_{b}", align_bytes=MX)
+            nc.scalar.activation(h_at_n5[:], h_win[b][:].indirect(n5_l[:]), ACT.Copy)
+            nw = sb.tile([P, S], F32, name=f"nw{b}")
+            nc.vector.tensor_tensor(nw[:], h_win[b][:, :S], h_at_n5[:], ALU.subtract)
+            return nw
+
+        def put_nw(b, nw, queue):
+            nc.scalar.activation(page[b][:].indirect(n4_l[:]), nw[:], ACT.Copy)
+            queue.dma_start(out=out[P * b : P * (b + 1), :], in_=page[b][:])
+
+        for u in range(2):
+            start, stop = HALF * u, HALF * (u + 1)
+            z_planes = sb.tile([P, PACK, HALF], BF16, name=f"z_planes{u}")
+            for t in range(PACK):
+                nc.vector.scalar_tensor_tensor(
+                    z_planes[:, t, :],
+                    gates[u][:, t, :],
+                    gs_t[:, t : t + 1],
+                    s_win[t][:, start:stop],
+                    ALU.mult,
+                    ALU.mult,
+                )
+            z_woven = sb.tile([P, HALF * PACK], BF16, name=f"z_woven{u}", align_bytes=MX)
+            nc.vector.tensor_copy(
+                z_woven[:].rearrange("p (c i t) -> p c t i", i=4, t=PACK),
+                z_planes[:].rearrange("p t (c i) -> p c t i", i=4),
+            )
+            nc.vector.quantize_mx(z_words[:, start:stop].bitcast(FP8X4), z_scales[:, start:stop], z_woven[:])
+            for b in range(2):
+                make_h(b, start, stop)
+
+        put_h(0, 0, HALF)
+        put_h(1, 0, HALF)
+        put_h(0, HALF, S)
+        nw0 = make_nw(0)
+        put_h(1, HALF, S)
+        pick_k1_bytes(1, "h_at_n5_0")
+        nw1 = make_nw(1)
+        k_words.append(pick_k1_words(1, "h_at_n5_1"))
+        put_nw(0, nw0, nc.gpsimd)
+        put_nw(1, nw1, nc.sync)
+        make_h(2, 0, S)
+        make_h(3, 0, S)
+        nw2 = make_nw(2)
+        put_h(2, 0, S)
+        nw3 = make_nw(3)
+        put_nw(2, nw2, nc.sync)
+        put_h(3, 0, S)
+        put_nw(3, nw3, nc.sync)

@@ -65,26 +65,26 @@ def tile_picked_hwqhopdpagq_none_p_kernel(
         d_rows_k1 = sb.tile([P, G], U8)
         x_placed = sb.tile([P, S], U8, align_bytes=MX)
         k_placed = [sb.tile([P, S], U8, name=f"k_placed{u}", align_bytes=MX) for u in range(2)]
-        for zeroed in [x_rows, d_rows_ci, d_rows_k1, x_placed] + k_placed:
+        for zeroed in [d_rows_ci, x_placed] + k_placed:
             nc.vector.memset(zeroed[:].bitcast(I32), 0)
+        for zeroed in [x_rows, d_rows_k1]:
+            nc.gpsimd.memset(zeroed[:].bitcast(I32), 0)
 
         s_win = [sb.tile([P, WIDE], F32, name=f"s_win{t}") for t in range(PACK)]
         st_win = [sb.tile([P, WIDE], F32, name=f"st_win{t}") for t in range(PACK)]
         h_win = [sb.tile([P, H_WIDE], F32, name=f"h_win{b}") for b in range(PACK)]
-        for win in s_win + st_win + h_win:
-            nc.vector.memset(win[:, S:], 0.0)
 
         offs_l = load_list(offs, "offs_l")
         ci_l = load_list(ci, "ci_l")
         nc.scalar.dma_start(out=x_rows[:].bitcast(I32)[0:P:8, :], in_=x_scales[0].bitcast(I32))
         for q in range(4):
-            nc.scalar.dma_start(
+            (nc.scalar if q < 2 else nc.sync).dma_start(
                 out=d_rows_ci[:].bitcast(I32)[32 * q : 32 * q + 4, :],
                 in_=d_scales[0].bitcast(I32)[4 * q : 4 * q + 4, :],
             )
         d_tab = sb.tile([P, G], U32)
         nc.sync.dma_start(out=d_tab[:].bitcast(I32), in_=d_words[0].rearrange("p n t -> p (n t)").bitcast(I32))
-        x_tab = sb.tile([P, T], U32)
+        x_tab = sb.tile([P, T], U32, tag="x_tab", align_bytes=MX)
         nc.sync.dma_start(out=x_tab[:].bitcast(I32), in_=x_words[0].rearrange("p n t -> p (n t)").bitcast(I32))
         n1_l = load_list(n1, "n1_l")
         k1_l = load_list(k1, "k1_l")
@@ -95,6 +95,10 @@ def tile_picked_hwqhopdpagq_none_p_kernel(
         n5_l = load_list(n5, "n5_l")
         n3_l = load_list(n3, "n3_l")
         n4_l = load_list(n4, "n4_l")
+
+        warm = sb.tile([P, 2], F32)
+        nc.vector.memset(warm[:, 0:1], 0.0)
+        nc.scalar.activation(warm[:, 1:2], warm[:, 0:1], ACT.Sigmoid)
 
         x_picked = sb.tile([P, S], U8)
         nc.vector.tensor_copy(x_picked[:], x_rows[:].indirect(offs_l[:]))
@@ -109,20 +113,26 @@ def tile_picked_hwqhopdpagq_none_p_kernel(
         )
         c_words = sb.tile([P, H], U32)
         nc.vector.tensor_copy(c_words[:], d_tab[:].indirect(ci_l[:]))
-        c_words_dealt = sb.tile([P, H], U32, align_bytes=MX)
-        nc.vector.tensor_copy(
-            c_words_dealt[:].rearrange("p (t c i) -> p c t i", t=PACK, i=4),
-            c_words[:].rearrange("p (c i t) -> p c t i", t=PACK, i=4),
-        )
+        c_words_by_t = c_words[:].rearrange("p (c i t) -> p c t i", t=PACK, i=4)
+        c_first = sb.tile([P, P], U32, align_bytes=MX)
+        nc.vector.tensor_copy(c_first[:].rearrange("p (c i) -> p c i", i=4), c_words_by_t[:, :, 0, :])
         xq_words = sb.tile([P, S], U32, align_bytes=MX)
         nc.vector.tensor_copy(xq_words[:], x_tab[:].indirect(offs_l[:]))
+        c_rest = sb.tile([P, (PACK - 1) * P], U32, tag="x_tab", align_bytes=MX)
+        nc.vector.tensor_copy(
+            c_rest[:].rearrange("p (t c i) -> p c t i", t=PACK - 1, i=4), c_words_by_t[:, :, 1:, :]
+        )
+        c_words_dealt = [c_first[:]] + [c_rest[:, P * t : P * (t + 1)] for t in range(PACK - 1)]
 
         s_at_n1 = sb.tile([P, PACK, S], F32, tag="looked_up")
         for t in range(PACK):
             cols = slice(P * t, P * (t + 1))
             acc = psum.tile([P, S], F32, name="acc")
-            product(nc, acc[:], c_words_dealt[:, cols], c_bytes_dealt[:, cols], xq_words[:], x_placed[:])
-            nc.vector.tensor_scalar(s_win[t][:, :S], acc[:], SIXTEENTH, None, ALU.mult)
+            product(nc, acc[:], c_words_dealt[t], c_bytes_dealt[:, cols], xq_words[:], x_placed[:])
+            if t == 0:
+                nc.scalar.activation(s_win[t][:, :S], acc[:], ACT.Copy, scale=SIXTEENTH)
+            else:
+                nc.vector.tensor_scalar(s_win[t][:, :S], acc[:], SIXTEENTH, None, ALU.mult)
             nc.scalar.activation(s_at_n1[:, t, :], s_win[t][:].indirect(n1_l[:]), ACT.Copy)
 
         def pick_k1_bytes(u, tag):
@@ -169,7 +179,10 @@ def tile_picked_hwqhopdpagq_none_p_kernel(
                 z_words[:, start:stop],
                 z_scales[:, start:stop],
             )
-            nc.vector.tensor_scalar(h_win[b][:, start:stop], acc[:, : stop - start], SIXTEENTH, None, ALU.mult)
+            if b == 0 and start == 0:
+                nc.scalar.activation(h_win[b][:, start:stop], acc[:, : stop - start], ACT.Copy, scale=SIXTEENTH)
+            else:
+                nc.vector.tensor_scalar(h_win[b][:, start:stop], acc[:, : stop - start], SIXTEENTH, None, ALU.mult)
 
         def put_h(b, start, stop):
             nc.scalar.activation(page[b][:].indirect(entries(n3_l, start, stop)), h_win[b][:, start:stop], ACT.Copy)
@@ -187,7 +200,7 @@ def tile_picked_hwqhopdpagq_none_p_kernel(
 
         for u in range(2):
             start, stop = HALF * u, HALF * (u + 1)
-            z_planes = sb.tile([P, PACK, HALF], BF16, name=f"z_planes{u}")
+            z_planes = sb.tile([P, PACK, HALF], BF16, name=f"z_planes{u}", tag=f"z_bf16_{u}", align_bytes=MX)
             for t in range(PACK):
                 nc.vector.scalar_tensor_tensor(
                     z_planes[:, t, :],
@@ -197,7 +210,7 @@ def tile_picked_hwqhopdpagq_none_p_kernel(
                     ALU.mult,
                     ALU.mult,
                 )
-            z_woven = sb.tile([P, HALF * PACK], BF16, name=f"z_woven{u}", align_bytes=MX)
+            z_woven = sb.tile([P, HALF * PACK], BF16, name=f"z_woven{u}", tag=f"z_bf16_{u + 1}", align_bytes=MX)
             nc.vector.tensor_copy(
                 z_woven[:].rearrange("p (c i t) -> p c t i", i=4, t=PACK),
                 z_planes[:].rearrange("p t (c i) -> p c t i", i=4),
@@ -205,16 +218,16 @@ def tile_picked_hwqhopdpagq_none_p_kernel(
             nc.vector.quantize_mx(z_words[:, start:stop].bitcast(FP8X4), z_scales[:, start:stop], z_woven[:])
             for b in range(2):
                 make_h(b, start, stop)
+        pick_k1_bytes(1, "z_bf16_2")
 
         put_h(0, 0, HALF)
         put_h(1, 0, HALF)
         put_h(0, HALF, S)
         nw0 = make_nw(0)
         put_h(1, HALF, S)
-        pick_k1_bytes(1, "h_at_n5_0")
+        k_words.append(pick_k1_words(1, "h_at_n5_0"))
         nw1 = make_nw(1)
-        k_words.append(pick_k1_words(1, "h_at_n5_1"))
-        put_nw(0, nw0, nc.gpsimd)
+        put_nw(0, nw0, nc.sync)
         put_nw(1, nw1, nc.sync)
         make_h(2, 0, S)
         make_h(3, 0, S)

@@ -53,6 +53,7 @@ def tile_picked_hwqhopdpagq_none_p_kernel(
     with ExitStack() as ctx:
         lists = ctx.enter_context(tc.tile_pool(name="lists", bufs=1))
         sb = ctx.enter_context(tc.tile_pool(name="sb", bufs=1))
+        shared = ctx.enter_context(tc.tile_pool(name="shared", bufs=1))
         psum = ctx.enter_context(tc.psum_pool(name="psum", bufs=8))
 
         def load_list(src, name):
@@ -64,8 +65,8 @@ def tile_picked_hwqhopdpagq_none_p_kernel(
         d_rows_ci = sb.tile([P, G], U8)
         d_rows_k1 = sb.tile([P, G], U8)
         x_placed = sb.tile([P, S], U8, align_bytes=MX)
-        k_placed = [sb.tile([P, S], U8, name=f"k_placed{u}", align_bytes=MX) for u in range(2)]
-        for zeroed in [d_rows_ci, x_placed] + k_placed:
+        k_placed = sb.tile([P, H], U8, align_bytes=MX)
+        for zeroed in [d_rows_ci, x_placed, k_placed]:
             nc.vector.memset(zeroed[:].bitcast(I32), 0)
         for zeroed in [x_rows, d_rows_k1]:
             nc.gpsimd.memset(zeroed[:].bitcast(I32), 0)
@@ -84,11 +85,11 @@ def tile_picked_hwqhopdpagq_none_p_kernel(
             )
         d_tab = sb.tile([P, G], U32)
         nc.sync.dma_start(out=d_tab[:].bitcast(I32), in_=d_words[0].rearrange("p n t -> p (n t)").bitcast(I32))
-        x_tab = sb.tile([P, T], U32, tag="x_tab", align_bytes=MX)
+        x_tab = shared.tile([P, T], U32, offset=0, align_bytes=MX)
         nc.sync.dma_start(out=x_tab[:].bitcast(I32), in_=x_words[0].rearrange("p n t -> p (n t)").bitcast(I32))
         n1_l = load_list(n1, "n1_l")
-        k1_l = load_list(k1, "k1_l")
         nc.sync.dma_start(out=d_rows_k1[:].bitcast(I32)[0:P:8, :], in_=d_scales[0].bitcast(I32))
+        k1_l = load_list(k1, "k1_l")
         n2_l = load_list(n2, "n2_l")
         gs_t = sb.tile([P, PACK], F32)
         nc.sync.dma_start(out=gs_t[:], in_=gs.rearrange("(p t) o -> p (t o)", t=PACK))
@@ -106,11 +107,9 @@ def tile_picked_hwqhopdpagq_none_p_kernel(
 
         c_bytes = sb.tile([P, H], U8)
         nc.vector.tensor_copy(c_bytes[:], d_rows_ci[:].indirect(ci_l[:]))
-        c_bytes_dealt = sb.tile([P, H], U8, align_bytes=MX)
-        nc.vector.tensor_copy(
-            c_bytes_dealt[:].rearrange("p (t c i) -> p c t i", t=PACK, i=16),
-            c_bytes[:].rearrange("p (c i t) -> p c t i", t=PACK, i=16),
-        )
+        c_bytes_by_t = c_bytes[:].rearrange("p (c i t) -> p c t i", t=PACK, i=16)
+        c_bytes_first = sb.tile([P, P], U8, align_bytes=MX)
+        nc.vector.tensor_copy(c_bytes_first[:].rearrange("p (c i) -> p c i", i=16), c_bytes_by_t[:, :, 0, :])
         c_words = sb.tile([P, H], U32)
         nc.vector.tensor_copy(c_words[:], d_tab[:].indirect(ci_l[:]))
         c_words_by_t = c_words[:].rearrange("p (c i t) -> p c t i", t=PACK, i=4)
@@ -118,42 +117,46 @@ def tile_picked_hwqhopdpagq_none_p_kernel(
         nc.vector.tensor_copy(c_first[:].rearrange("p (c i) -> p c i", i=4), c_words_by_t[:, :, 0, :])
         xq_words = sb.tile([P, S], U32, align_bytes=MX)
         nc.vector.tensor_copy(xq_words[:], x_tab[:].indirect(offs_l[:]))
-        c_rest = sb.tile([P, (PACK - 1) * P], U32, tag="x_tab", align_bytes=MX)
+        c_rest = shared.tile([P, (PACK - 1) * P], U32, offset=0, align_bytes=MX)
         nc.vector.tensor_copy(
             c_rest[:].rearrange("p (t c i) -> p c t i", t=PACK - 1, i=4), c_words_by_t[:, :, 1:, :]
         )
+        c_bytes_rest = shared.tile([P, (PACK - 1) * P], U8, offset=2048, align_bytes=MX)
+        nc.vector.tensor_copy(
+            c_bytes_rest[:].rearrange("p (t c i) -> p c t i", t=PACK - 1, i=16), c_bytes_by_t[:, :, 1:, :]
+        )
+        c_bytes_dealt = [c_bytes_first[:]] + [c_bytes_rest[:, P * t : P * (t + 1)] for t in range(PACK - 1)]
         c_words_dealt = [c_first[:]] + [c_rest[:, P * t : P * (t + 1)] for t in range(PACK - 1)]
 
+        s_acc = []
         s_at_n1 = sb.tile([P, PACK, S], F32, tag="looked_up")
         for t in range(PACK):
-            cols = slice(P * t, P * (t + 1))
             acc = psum.tile([P, S], F32, name="acc")
-            product(nc, acc[:], c_words_dealt[t], c_bytes_dealt[:, cols], xq_words[:], x_placed[:])
+            s_acc.append(acc)
+            product(nc, acc[:], c_words_dealt[t], c_bytes_dealt[t], xq_words[:], x_placed[:])
             if t == 0:
                 nc.scalar.activation(s_win[t][:, :S], acc[:], ACT.Copy, scale=SIXTEENTH)
             else:
                 nc.vector.tensor_scalar(s_win[t][:, :S], acc[:], SIXTEENTH, None, ALU.mult)
             nc.scalar.activation(s_at_n1[:, t, :], s_win[t][:].indirect(n1_l[:]), ACT.Copy)
 
-        def pick_k1_bytes(u, tag):
-            picked = sb.tile([P, S], U8, name=f"k_picked{u}", tag=tag, align_bytes=MX)
-            nc.vector.tensor_copy(picked[:], d_rows_k1[:].indirect(entries(k1_l, S * u, S * (u + 1))))
-            place_scale_rows(nc.sync, k_placed[u], picked)
-
         def pick_k1_words(u, tag):
             picked = sb.tile([P, S], U32, name=f"k_words{u}", tag=tag, align_bytes=MX)
             nc.vector.tensor_copy(picked[:], d_tab[:].indirect(entries(k1_l, S * u, S * (u + 1))))
             return picked
 
-        def subtract_s(t):
-            nc.vector.tensor_tensor(st_win[t][:, :S], s_at_n1[:, t, :], s_win[t][:, :S], ALU.subtract)
-
-        pick_k1_bytes(0, "k_picked0")
-        subtract_s(0)
-        subtract_s(1)
+        k_picked = sb.tile([P, H], U8)
+        nc.vector.tensor_copy(k_picked[:], d_rows_k1[:].indirect(k1_l[:]))
+        place_scale_rows(nc.sync, k_placed, k_picked)
         k_words = [pick_k1_words(0, "k_words0")]
-        subtract_s(2)
-        subtract_s(3)
+        for t in range(PACK - 1):
+            nc.gpsimd.tensor_tensor(st_win[t][:, :S], s_at_n1[:, t, :], s_win[t][:, :S], ALU.subtract)
+        last = PACK - 1
+        nc.vector.scalar_tensor_tensor(
+            st_win[last][:, :S], s_acc[last][:], -SIXTEENTH, s_at_n1[:, last, :], ALU.mult, ALU.add
+        )
+        gs16 = sb.tile([P, PACK], F32)
+        nc.vector.tensor_scalar(gs16[:], gs_t[:], SIXTEENTH, None, ALU.mult)
 
         gates = []
         for u, tag in enumerate(["gate0", "looked_up"]):
@@ -175,7 +178,7 @@ def tile_picked_hwqhopdpagq_none_p_kernel(
                 nc,
                 acc[:, : stop - start],
                 k_words[b // 2][:, cols],
-                k_placed[b // 2][:, cols],
+                k_placed[:, P * b : P * (b + 1)],
                 z_words[:, start:stop],
                 z_scales[:, start:stop],
             )
@@ -204,9 +207,9 @@ def tile_picked_hwqhopdpagq_none_p_kernel(
             for t in range(PACK):
                 nc.vector.scalar_tensor_tensor(
                     z_planes[:, t, :],
+                    s_acc[t][:, start:stop],
+                    gs16[:, t : t + 1],
                     gates[u][:, t, :],
-                    gs_t[:, t : t + 1],
-                    s_win[t][:, start:stop],
                     ALU.mult,
                     ALU.mult,
                 )
@@ -218,7 +221,6 @@ def tile_picked_hwqhopdpagq_none_p_kernel(
             nc.vector.quantize_mx(z_words[:, start:stop].bitcast(FP8X4), z_scales[:, start:stop], z_woven[:])
             for b in range(2):
                 make_h(b, start, stop)
-        pick_k1_bytes(1, "z_bf16_2")
 
         put_h(0, 0, HALF)
         put_h(1, 0, HALF)

@@ -66,10 +66,8 @@ def tile_picked_hwqhopdpagq_none_p_kernel(
         d_rows_k1 = sb.tile([P, G], U8)
         x_placed = sb.tile([P, S], U8, align_bytes=MX)
         k_placed = sb.tile([P, H], U8, align_bytes=MX)
-        for zeroed in [d_rows_ci, x_placed, k_placed]:
+        for zeroed in [d_rows_ci, x_rows, d_rows_k1, x_placed, k_placed]:
             nc.vector.memset(zeroed[:].bitcast(I32), 0)
-        for zeroed in [x_rows, d_rows_k1]:
-            nc.gpsimd.memset(zeroed[:].bitcast(I32), 0)
 
         s_win = [sb.tile([P, WIDE], F32, name=f"s_win{t}") for t in range(PACK)]
         st_win = [sb.tile([P, WIDE], F32, name=f"st_win{t}") for t in range(PACK)]
@@ -79,7 +77,7 @@ def tile_picked_hwqhopdpagq_none_p_kernel(
         ci_l = load_list(ci, "ci_l")
         nc.scalar.dma_start(out=x_rows[:].bitcast(I32)[0:P:8, :], in_=x_scales[0].bitcast(I32))
         for q in range(4):
-            (nc.scalar if q < 2 else nc.sync).dma_start(
+            (nc.scalar if q == 0 else nc.sync).dma_start(
                 out=d_rows_ci[:].bitcast(I32)[32 * q : 32 * q + 4, :],
                 in_=d_scales[0].bitcast(I32)[4 * q : 4 * q + 4, :],
             )

from contextlib import ExitStack

import concourse.mybir as mybir

F32 = mybir.dt.float32
BF16 = mybir.dt.bfloat16
I32 = mybir.dt.int32
U32 = mybir.dt.uint32
U16 = mybir.dt.uint16
U8 = mybir.dt.uint8
FP8X4 = mybir.dt.float8_e4m3fn_x4
ALU = mybir.AluOpType
ACT = mybir.ActivationFunctionType

P = 128
PACK = 4
T, S, G, H, U = 1024, 256, 2048, 512, 512
HALF = S // 2
PER_COL = 16
WIDE = 2 * S
H_WIDE = S + 16
SIXTEENTH = 0.0625
MX = 64

FLOPS = 2 * 2 * 512 * H * S


def entries(lst, start, stop):
    return lst[:, start // PER_COL : stop // PER_COL]


def place_scale_rows(queue, placed, picked):
    for r in range(4):
        queue.dma_start(out=placed[:].bitcast(I32)[r:P:32, :], in_=picked[:].bitcast(I32)[8 * r : P : 32, :])


def product(nc, acc, words, scales, moving, moving_scales):
    nc.tensor.matmul_mx(
        out=acc,
        lhsT=words.bitcast(FP8X4),
        lhsT_scale=scales,
        rhs=moving.bitcast(FP8X4),
        rhs_scale=moving_scales,
        start=True,
        stop=True,
    )


def tile_picked_hwqhopdpagq_none_p_kernel(
    tc, x_words, x_scales, d_words, d_scales, gs, offs, ci, n1, n2, k1, n3, n4, n5, out
):
    nc = tc.nc
    with ExitStack() as ctx:
        lists = ctx.enter_context(tc.tile_pool(name="lists", bufs=1))
        sb = ctx.enter_context(tc.tile_pool(name="sb", bufs=1))
        shared = ctx.enter_context(tc.tile_pool(name="shared", bufs=1))
        psum = ctx.enter_context(tc.psum_pool(name="psum", bufs=8))

        def load_list(src, name):
            lst = lists.tile(list(src.shape), U16, name=name)
            nc.sync.dma_start(lst[:], src)
            return lst

        x_rows = sb.tile([P, T], U8)
        d_rows_ci = sb.tile([P, G], U8)
        d_rows_k1 = sb.tile([P, G], U8)
        x_placed = sb.tile([P, S], U8, align_bytes=MX)
        k_placed = sb.tile([P, H], U8, align_bytes=MX)
        for zeroed in [d_rows_ci, x_rows, d_rows_k1, x_placed, k_placed]:
            nc.vector.memset(zeroed[:].bitcast(I32), 0)

        s_win = [sb.tile([P, WIDE], F32, name=f"s_win{t}") for t in range(PACK)]
        st_win = [sb.tile([P, WIDE], F32, name=f"st_win{t}") for t in range(PACK)]
        h_win = [sb.tile([P, H_WIDE], F32, name=f"h_win{b}") for b in range(PACK)]

        offs_l = load_list(offs, "offs_l")
        ci_l = load_list(ci, "ci_l")
        nc.scalar.dma_start(out=x_rows[:].bitcast(I32)[0:P:8, :], in_=x_scales[0].bitcast(I32))
        for q in range(4):
            (nc.scalar if q == 0 else nc.sync).dma_start(
                out=d_rows_ci[:].bitcast(I32)[32 * q : 32 * q + 4, :],
                in_=d_scales[0].bitcast(I32)[4 * q : 4 * q + 4, :],
            )
        d_tab = sb.tile([P, G], U32)
        nc.sync.dma_start(out=d_tab[:].bitcast(I32), in_=d_words[0].rearrange("p n t -> p (n t)").bitcast(I32))
        x_tab = shared.tile([P, T], U32, offset=0, align_bytes=MX)
        nc.sync.dma_start(out=x_tab[:].bitcast(I32), in_=x_words[0].rearrange("p n t -> p (n t)").bitcast(I32))
        n1_l = load_list(n1, "n1_l")
        nc.sync.dma_start(out=d_rows_k1[:].bitcast(I32)[0:P:8, :], in_=d_scales[0].bitcast(I32))
        k1_l = load_list(k1, "k1_l")
        n2_l = load_list(n2, "n2_l")
        gs_t = sb.tile([P, PACK], F32)
        nc.sync.dma_start(out=gs_t[:], in_=gs.rearrange("(p t) o -> p (t o)", t=PACK))
        n5_l = load_list(n5, "n5_l")
        n3_l = load_list(n3, "n3_l")
        n4_l = load_list(n4, "n4_l")

        warm = sb.tile([P, 2], F32)
        nc.vector.memset(warm[:, 0:1], 0.0)
        nc.scalar.activation(warm[:, 1:2], warm[:, 0:1], ACT.Sigmoid)

        x_picked = sb.tile([P, S], U8)
        nc.vector.tensor_copy(x_picked[:], x_rows[:].indirect(offs_l[:]))
        place_scale_rows(nc.scalar, x_placed, x_picked)

        c_bytes = sb.tile([P, H], U8)
        nc.vector.tensor_copy(c_bytes[:], d_rows_ci[:].indirect(ci_l[:]))
        c_bytes_by_t = c_bytes[:].rearrange("p (c i t) -> p c t i", t=PACK, i=16)
        c_bytes_first = sb.tile([P, P], U8, align_bytes=MX)
        nc.vector.tensor_copy(c_bytes_first[:].rearrange("p (c i) -> p c i", i=16), c_bytes_by_t[:, :, 0, :])
        c_words = sb.tile([P, H], U32)
        nc.vector.tensor_copy(c_words[:], d_tab[:].indirect(ci_l[:]))
        c_words_by_t = c_words[:].rearrange("p (c i t) -> p c t i", t=PACK, i=4)
        c_first = sb.tile([P, P], U32, align_bytes=MX)
        nc.vector.tensor_copy(c_first[:].rearrange("p (c i) -> p c i", i=4), c_words_by_t[:, :, 0, :])
        xq_words = sb.tile([P, S], U32, align_bytes=MX)
        nc.vector.tensor_copy(xq_words[:], x_tab[:].indirect(offs_l[:]))
        c_rest = shared.tile([P, (PACK - 1) * P], U32, offset=0, align_bytes=MX)
        nc.vector.tensor_copy(
            c_rest[:].rearrange("p (t c i) -> p c t i", t=PACK - 1, i=4), c_words_by_t[:, :, 1:, :]
        )
        c_bytes_rest = shared.tile([P, (PACK - 1) * P], U8, offset=2048, align_bytes=MX)
        nc.vector.tensor_copy(
            c_bytes_rest[:].rearrange("p (t c i) -> p c t i", t=PACK - 1, i=16), c_bytes_by_t[:, :, 1:, :]
        )
        c_bytes_dealt = [c_bytes_first[:]] + [c_bytes_rest[:, P * t : P * (t + 1)] for t in range(PACK - 1)]
        c_words_dealt = [c_first[:]] + [c_rest[:, P * t : P * (t + 1)] for t in range(PACK - 1)]

        s_acc = []
        s_at_n1 = sb.tile([P, PACK, S], F32, tag="looked_up")
        for t in range(PACK):
            acc = psum.tile([P, S], F32, name="acc")
            s_acc.append(acc)
            product(nc, acc[:], c_words_dealt[t], c_bytes_dealt[t], xq_words[:], x_placed[:])
            if t == 0:
                nc.scalar.activation(s_win[t][:, :S], acc[:], ACT.Copy, scale=SIXTEENTH)
            else:
                nc.vector.tensor_scalar(s_win[t][:, :S], acc[:], SIXTEENTH, None, ALU.mult)
            nc.scalar.activation(s_at_n1[:, t, :], s_win[t][:].indirect(n1_l[:]), ACT.Copy)

        def pick_k1_words(u, tag):
            picked = sb.tile([P, S], U32, name=f"k_words{u}", tag=tag, align_bytes=MX)
            nc.vector.tensor_copy(picked[:], d_tab[:].indirect(entries(k1_l, S * u, S * (u + 1))))
            return picked

        k_picked = sb.tile([P, H], U8)
        nc.vector.tensor_copy(k_picked[:], d_rows_k1[:].indirect(k1_l[:]))
        place_scale_rows(nc.sync, k_placed, k_picked)
        k_words = [pick_k1_words(0, "k_words0")]
        for t in range(PACK - 1):
            nc.gpsimd.tensor_tensor(st_win[t][:, :S], s_at_n1[:, t, :], s_win[t][:, :S], ALU.subtract)
        last = PACK - 1
        nc.vector.scalar_tensor_tensor(
            st_win[last][:, :S], s_acc[last][:], -SIXTEENTH, s_at_n1[:, last, :], ALU.mult, ALU.add
        )
        gs16 = sb.tile([P, PACK], F32)
        nc.vector.tensor_scalar(gs16[:], gs_t[:], SIXTEENTH, None, ALU.mult)

        gates = []
        for u, tag in enumerate(["gate0", "looked_up"]):
            gate = sb.tile([P, PACK, HALF], F32, name=f"gate{u}", tag=tag)
            for t in range(PACK):
                nc.scalar.activation(
                    gate[:, t, :], st_win[t][:].indirect(entries(n2_l, HALF * u, HALF * (u + 1))), ACT.Sigmoid
                )
            gates.append(gate)

        z_words = sb.tile([P, S], U32, align_bytes=MX)
        z_scales = sb.tile([P, S], U8, align_bytes=MX)
        page = [sb.tile([P, U], F32, name=f"page{b}") for b in range(PACK)]

        def make_h(b, start, stop):
            cols = slice(P * (b % 2), P * (b % 2 + 1))
            acc = psum.tile([P, S], F32, name="acc")
            product(
                nc,
                acc[:, : stop - start],
                k_words[b // 2][:, cols],
                k_placed[:, P * b : P * (b + 1)],
                z_words[:, start:stop],
                z_scales[:, start:stop],
            )
            if b == 0 and start == 0:
                nc.scalar.activation(h_win[b][:, start:stop], acc[:, : stop - start], ACT.Copy, scale=SIXTEENTH)
            else:
                nc.vector.tensor_scalar(h_win[b][:, start:stop], acc[:, : stop - start], SIXTEENTH, None, ALU.mult)

        def put_h(b, start, stop):
            nc.scalar.activation(page[b][:].indirect(entries(n3_l, start, stop)), h_win[b][:, start:stop], ACT.Copy)

        def make_nw(b):
            h_at_n5 = sb.tile([P, S], F32, name=f"h_at_n5_{b}", tag=f"h_at_n5_{b}", align_bytes=MX)
            nc.scalar.activation(h_at_n5[:], h_win[b][:].indirect(n5_l[:]), ACT.Copy)
            nw = sb.tile([P, S], F32, name=f"nw{b}")
            nc.vector.tensor_tensor(nw[:], h_win[b][:, :S], h_at_n5[:], ALU.subtract)
            return nw

        def put_nw(b, nw, queue):
            nc.scalar.activation(page[b][:].indirect(n4_l[:]), nw[:], ACT.Copy)
            queue.dma_start(out=out[P * b : P * (b + 1), :], in_=page[b][:])

        for u in range(2):
            start, stop = HALF * u, HALF * (u + 1)
            z_planes = sb.tile([P, PACK, HALF], BF16, name=f"z_planes{u}", tag=f"z_bf16_{u}", align_bytes=MX)
            for t in range(PACK):
                nc.vector.scalar_tensor_tensor(
                    z_planes[:, t, :],
                    s_acc[t][:, start:stop],
                    gs16[:, t : t + 1],
                    gates[u][:, t, :],
                    ALU.mult,
                    ALU.mult,
                )
            z_woven = sb.tile([P, HALF * PACK], BF16, name=f"z_woven{u}", tag=f"z_bf16_{u + 1}", align_bytes=MX)
            nc.vector.tensor_copy(
                z_woven[:].rearrange("p (c i t) -> p c t i", i=4, t=PACK),
                z_planes[:].rearrange("p t (c i) -> p c t i", i=4),
            )
            nc.vector.quantize_mx(z_words[:, start:stop].bitcast(FP8X4), z_scales[:, start:stop], z_woven[:])
            for b in range(2):
                make_h(b, start, stop)

        put_h(0, 0, HALF)
        put_h(1, 0, HALF)
        put_h(0, HALF, S)
        nw0 = make_nw(0)
        put_h(1, HALF, S)
        k_words.append(pick_k1_words(1, "h_at_n5_0"))
        nw1 = make_nw(1)
        put_nw(0, nw0, nc.sync)
        put_nw(1, nw1, nc.sync)
        make_h(2, 0, S)
        make_h(3, 0, S)
        nw2 = make_nw(2)
        put_h(2, 0, S)
        nw3 = make_nw(3)
        put_nw(2, nw2, nc.sync)
        put_h(3, 0, S)
        put_nw(3, nw3, nc.sync)
